import numpy as np
import ml_dtypes


def mxq(x, axis, fmt="e4m3"):
    dtype, down = {"e4m3": (ml_dtypes.float8_e4m3fn, 7), "e5m2": (ml_dtypes.float8_e5m2, 14)}[fmt]
    v = np.moveaxis(np.asarray(x, np.float32).astype(ml_dtypes.bfloat16).astype(np.float64), axis, -1)
    blocks = v.reshape(v.shape[:-1] + (-1, 32))
    amax = np.abs(blocks).max(-1, keepdims=True)
    byte = np.maximum(np.where(amax > 0, np.frexp(amax)[1] - 1 + 127, 0) - down, 1)
    scale = np.exp2(byte - 127.0)
    codes = (blocks / scale).astype(np.float32).astype(dtype).astype(np.float64)
    return np.moveaxis((codes * scale).reshape(v.shape), -1, axis)


WIDE = False


def mx_kscale(k):
    if not WIDE:
        return np.ones(k)
    levels = np.array([10, -10, 5, -5, 0])
    if k % 512:
        return np.exp2(np.random.permutation(np.resize(levels, k // 32))).repeat(32)
    a = np.empty((k // 512, 16))
    for p in range(k // 512):
        a[p, :8] = np.random.permutation(np.resize(levels, 8))
        for g in range(8):
            far = levels[np.abs(levels - a[p, g]) >= 10]
            a[p, g + 8] = far[np.random.randint(len(far))]
    return np.exp2(a.ravel()).repeat(32)


def f64(x):
    return np.asarray(x).astype(np.float64)


def striped(idx):
    return np.tile(idx.reshape(-1, 16).T, (8, 1)).astype(np.uint16)


def unstriped(offs):
    return offs[:16].T.reshape(-1).astype(np.int64)


def striped8(idx):
    return np.concatenate([x.reshape(-1, 16).T for x in idx]).astype(np.uint16)


def runs(offs, k):
    lists = np.stack([offs[16 * r : 16 * r + 16].T.reshape(-1) for r in range(8)]).astype(np.int64)
    return lists[np.arange(k) % 512 // 64]


def pack_weight(w):
    k, n = w.shape
    w = f64(np.asarray(w, np.float32).astype(ml_dtypes.bfloat16)).reshape(k // 32, 32, n)
    amax = np.abs(w).max(1)
    byte = np.clip(np.where(amax > 0, np.frexp(amax)[1] - 1 + 127 - 7, 1), 1, 254)
    scaled = (w * np.exp2(127.0 - byte)[:, None, :]).reshape(k, n).astype(np.float32)
    words = np.ascontiguousarray(scaled.reshape(k // 512, 128, 4, n).transpose(0, 1, 3, 2)).astype(ml_dtypes.float8_e4m3fn).view(np.uint8)
    return words, np.ascontiguousarray(byte.astype(np.uint8).reshape(k // 512, 16, n))


def unpack_weight(words, scales):
    g, p, n, _ = words.shape
    vals = np.ascontiguousarray(words).view(ml_dtypes.float8_e4m3fn).astype(np.float64) * np.repeat(np.exp2(scales.astype(np.float64) - 127.0), 8, axis=1)[..., None]
    return vals.transpose(0, 1, 3, 2).reshape(g * 512, n)

def planes(y):
    n, m = y.shape
    v = y.astype(np.float32).astype(ml_dtypes.bfloat16).astype(np.float64).reshape(n // 32, 32, m)
    top = np.abs(v).max(1)
    byte = np.clip(np.where(top > 0, np.frexp(top)[1] - 1 + 127 - 7, 1), 1, 254)
    codes = (v * np.exp2(127.0 - byte)[:, None, :]).reshape(n, m).astype(np.float32).astype(ml_dtypes.float8_e4m3fn).view(np.uint8)
    words = codes.reshape(n // 512, 128, 4, m).transpose(0, 1, 3, 2)
    return np.ascontiguousarray(words), np.ascontiguousarray(byte.astype(np.uint8).reshape(n // 512, 16, m))


K, T, S, N, H, W = 512, 2048, 512, 512, 512, 256


def setup_inputs():
    n = np.random.standard_normal
    s = mx_kscale(K)[:, None]
    u = mx_kscale(S)
    packed_xT = pack_weight(n((K, T)) * s)
    perm = np.stack([np.random.permutation(H) for _ in range(8)])
    return {
        "x_words": packed_xT[0],
        "x_scales": packed_xT[1],
        "wa": (n((K, H)) / np.sqrt(K) / s).astype(np.float32),
        "wb": (n((K, N)) / np.sqrt(K) / s).astype(np.float32),
        "gt": (np.random.uniform(0.5, 1.5, (S, 1)) * u[:, None]).astype(np.float32),
        "gi": (np.random.uniform(0.5, 1.5, (S, 1)) / u[:, None]).astype(np.float32),
        "offs": striped(np.random.permutation(T)[:S]),
        "two": striped(np.random.permutation(T)[:S]),
        "n1": striped8(perm[:, :W]),
        "n2": striped8(perm[:, W:]),
        "n3": striped8(np.stack([np.random.permutation(N) for _ in range(8)])),
        "n4": striped8(np.stack([np.random.permutation(N) for _ in range(8)])),
        "n5": striped8(np.stack([np.random.permutation(N) for _ in range(8)])),
        "n6": striped8(np.stack([np.random.permutation(N) for _ in range(8)])),
        "n7": striped8(np.stack([np.random.permutation(N) for _ in range(8)])),
    }


def reference(x_words, x_scales, wa, wb, gt, gi, offs, two, n1, n2, n3, n4, n5, n6, n7):
    xq = unpack_weight(x_words, x_scales)[:, unstriped(offs)]
    a = xq.T @ mxq(f64(wa), 0, "e4m3")
    pa = a[np.arange(S)[:, None], runs(n1, S)]
    pb = a[np.arange(S)[:, None], runs(n2, S)]
    rb = pa * pb
    ra = pa + pb
    ds = np.zeros((S, H))
    ds[np.arange(S)[:, None], runs(n1, S)] = ra
    dt = ds.copy()
    dt[np.arange(S)[:, None], runs(n2, S)] = rb
    z = f64(gt) * dt
    x_two = unpack_weight(x_words, x_scales)[:, unstriped(two)]
    b = x_two.T @ mxq(f64(wb), 0, "e4m3")
    z2 = f64(gi) * (b + b[np.arange(S)[:, None], runs(n3, S)] - (np.maximum(b[np.arange(S)[:, None], runs(n4, S)], b[np.arange(S)[:, None], runs(n5, S)])))
    cv = 0.0625 * ((mxq(z, 0, "e4m3").T @ mxq(z2, 0, "e4m3")))
    out_0 = 0.75 * (cv[np.arange(H)[:, None], runs(n6, H)] + cv[np.arange(H)[:, None], runs(n7, H)]) - cv
    return (out_0,) + planes(out_0)

@@ -1,0 +1,243 @@
+from contextlib import ExitStack
+
+import concourse.mybir as mybir
+
+K, T, S, H, N, W = 512, 2048, 512, 512, 512, 256
+FLOPS = 2 * K * S * H + 2 * K * S * N + 2 * S * H * N
+
+F32 = mybir.dt.float32
+BF16 = mybir.dt.bfloat16
+I32 = mybir.dt.int32
+U32 = mybir.dt.uint32
+U16 = mybir.dt.uint16
+U8 = mybir.dt.uint8
+FP8X4 = mybir.dt.float8_e4m3fn_x4
+ADD = mybir.AluOpType.add
+SUB = mybir.AluOpType.subtract
+MULT = mybir.AluOpType.mult
+MAX = mybir.AluOpType.max
+COPY = mybir.ActivationFunctionType.Copy
+
+P = 128
+PACK = 4
+LIST_ROWS = 16
+PIECES = ((0, 256), (256, 384), (384, 512))
+
+
+def tile_picked_mombbondtrimlap_none_po_kernel(tc, x_words, x_scales, wa, wb, gt, gi, offs, two, n1, n2, n3, n4, n5, n6, n7, out_0, out_1, out_2):
+    nc = tc.nc
+    with ExitStack() as ctx:
+        keep = ctx.enter_context(tc.tile_pool(name="keep", bufs=1))
+        work = ctx.enter_context(tc.tile_pool(name="work", bufs=2))
+        psum = ctx.enter_context(tc.psum_pool(name="psum", bufs=1))
+
+        def load_list(name, src):
+            tile = keep.tile(list(src.shape), U16, name=name)
+            nc.sync.dma_start(tile[:], src)
+            return tile
+
+        def entries(tile, lo, hi):
+            return tile[:, lo // LIST_ROWS : hi // LIST_ROWS]
+
+        xs = keep.tile([P, T], U8, name="xs")
+        for q in range(4):
+            rows = x_scales[0, 4 * q : 4 * q + 4, :].bitcast(I32)
+            nc.scalar.dma_start(xs[32 * q : 32 * q + 32, :].bitcast(I32), rows.unsqueeze(0).to_broadcast([8, 4, T // 4]))
+        offs_sb = load_list("offs_sb", offs)
+        two_sb = load_list("two_sb", two)
+        wa_rows = wa.rearrange("(p j) c -> p j c", j=PACK)
+        wa_raw = [keep.tile([P, PACK, H // 2], F32, name=f"wa_raw{h}") for h in range(2)]
+        for h in range(2):
+            nc.sync.dma_start(wa_raw[h][:], wa_rows[:, :, h * (H // 2) : (h + 1) * (H // 2)])
+        xw = keep.tile([P, T], I32, name="xw")
+        nc.sync.dma_start(xw[:], x_words[0].rearrange("p n t -> p (n t)").bitcast(I32))
+        n1_sb = load_list("n1_sb", n1)
+        n2_sb = load_list("n2_sb", n2)
+        wb_raw = keep.tile([P, PACK, N], F32, name="wb_raw")
+        nc.sync.dma_start(wb_raw[:], wb.rearrange("(p j) c -> p j c", j=PACK))
+
+        def load_weights(name, src):
+            tiles = []
+            for t in range(PACK):
+                tile = keep.tile([P, 1], F32, name=f"{name}{t}")
+                with nc.allow_non_contiguous_dma(reason="one weight for each partition"):
+                    nc.sync.dma_start(tile[:], src.rearrange("(q t e) o -> t q e o", t=PACK, e=8)[t])
+                tiles.append(tile)
+            return tiles
+
+        gt_sb = load_weights("gt_sb", gt)
+        n4_sb = load_list("n4_sb", n4)
+        n5_sb = load_list("n5_sb", n5)
+        n3_sb = load_list("n3_sb", n3)
+        gi_sb = load_weights("gi_sb", gi)
+        n6_sb = load_list("n6_sb", n6)
+        n7_sb = load_list("n7_sb", n7)
+
+        def pick_scales(name, lst):
+            got = keep.tile([P, S], U8, name=name + "_got")
+            nc.vector.tensor_copy(got[:], xs[:].indirect(lst[:]))
+            dealt = keep.tile([P, S], U8, name=name + "_dealt", align_bytes=64)
+            nc.vector.tensor_copy(
+                dealt[:].bitcast(I32).rearrange("p (t q w) -> p q t w", t=PACK, w=2),
+                got[:].bitcast(I32).rearrange("p (q t w) -> p q t w", t=PACK, w=2),
+            )
+            return dealt
+
+        def pick_words(name, lst):
+            dealt = keep.tile([P, S], U32, name=name, align_bytes=64)
+            nc.vector.tensor_copy(
+                dealt[:].rearrange("p (t q e) -> p q t e", t=PACK, e=8),
+                xw[:].bitcast(U32).indirect(lst[:]),
+            )
+            return dealt
+
+        def interleave(dst, raw):
+            nc.scalar.copy(
+                dst.rearrange("p (c i j) -> p c j i", i=4, j=PACK),
+                raw.rearrange("p j (c i) -> p c j i", i=4),
+            )
+
+        def quantize(words, scales, grouped, lo, hi):
+            nc.vector.quantize_mx(
+                out=words[:, lo:hi].bitcast(FP8X4), scales=scales[:, lo:hi], in_=grouped[:, PACK * lo : PACK * hi]
+            )
+
+        def product(acc, l_words, l_scales, t, r_words, r_scales, lo, hi):
+            cols = slice(t * P, (t + 1) * P)
+            nc.tensor.matmul_mx(
+                out=acc[:, lo:hi],
+                lhsT=l_words[:, cols].bitcast(FP8X4),
+                lhsT_scale=l_scales[:, cols],
+                rhs=r_words[:, lo:hi].bitcast(FP8X4),
+                rhs_scale=r_scales[:, lo:hi],
+                start=True,
+                stop=True,
+            )
+
+        def mx_tiles(name, tag=None):
+            grouped = keep.tile([P, PACK * N], BF16, name=name + "_bf", tag=tag or name + "_bf", align_bytes=64)
+            words = keep.tile([P, N], U32, name=name + "_words", align_bytes=64)
+            scales = keep.tile([P, N], U8, name=name + "_scales", align_bytes=64)
+            return grouped, words, scales
+
+        xa_scales = pick_scales("xa_s", offs_sb)
+        xb_scales = pick_scales("xb_s", two_sb)
+        wa_bf, wa_words, wa_scales = mx_tiles("wa")
+        for h in range(2):
+            lo, hi = h * (H // 2), (h + 1) * (H // 2)
+            interleave(wa_bf[:, PACK * lo : PACK * hi], wa_raw[h][:])
+            quantize(wa_words, wa_scales, wa_bf, lo, hi)
+        xa_words = pick_words("xa_w", offs_sb)
+        xb_words = pick_words("xb_w", two_sb)
+
+        a_sb = [keep.tile([P, H], F32, name=f"a{t}") for t in range(PACK)]
+        for t in range(PACK):
+            acc = psum.tile([P, H], F32, name=f"acc_a{t}", tag=f"bank{t}")
+            product(acc, xa_words, xa_scales, t, wa_words, wa_scales, 0, H)
+            nc.scalar.copy(a_sb[t][:], acc[:])
+
+        wb_bf, wb_words, wb_scales = mx_tiles("wb", tag="wb_then_pa")
+        interleave(wb_bf[:], wb_raw[:])
+        z_bf, z_words, z_scales = mx_tiles("z")
+        z_view = z_bf[:].rearrange("p (t m j) -> p m t j", t=PACK, j=PACK)
+
+        def a_pair(tiles):
+            pa, pb, dt = {}, {}, {}
+            for t in tiles:
+                if t == 2:
+                    pa[t] = keep.tile([P, W], F32, name="pa2", tag="wb_then_pa", align_bytes=64)
+                else:
+                    pa[t] = work.tile([P, W], F32, name="pa")
+                nc.vector.tensor_copy(pa[t][:], a_sb[t][:].indirect(n1_sb[:]))
+                pb[t] = work.tile([P, W], F32, name="pb")
+                nc.vector.tensor_copy(pb[t][:], a_sb[t][:].indirect(n2_sb[:]))
+            for t in tiles:
+                dt[t] = work.tile([P, H], F32, name="dt")
+                nc.vector.tensor_tensor(dt[t][:].indirect(n1_sb[:]), pa[t][:], pb[t][:], ADD)
+            for t in tiles:
+                nc.vector.tensor_tensor(dt[t][:].indirect(n2_sb[:]), pa[t][:], pb[t][:], MULT)
+            for t in tiles:
+                nc.scalar.activation(
+                    z_view[:, :, :, t], dt[t][:].rearrange("p (m t) -> p m t", t=PACK), COPY, scale=gt_sb[t][:]
+                )
+
+        a_pair((0, 1))
+        quantize(wb_words, wb_scales, wb_bf, 0, N)
+        b_win = [keep.tile([P, 2 * N if t < 2 else N], F32, name=f"b_win{t}") for t in range(PACK)]
+        b_rest = keep.tile([P, 2 * N], F32, name="b_rest")
+        b_plain = [b_win[1][:, N:], b_win[0][:, N:], b_rest[:, :N], b_rest[:, N:]]
+        for t in range(PACK):
+            acc = psum.tile([P, N], F32, name=f"acc_b{t}", tag=f"bank{4 + t}")
+            product(acc, xb_words, xb_scales, t, wb_words, wb_scales, 0, N)
+            nc.scalar.copy(b_win[t][:, :N], acc[:])
+            nc.scalar.copy(b_plain[t], acc[:])
+        a_pair((2, 3))
+
+        z2_bf, z2_words, z2_scales = mx_tiles("z2")
+        z2_view = z2_bf[:].rearrange("p (c j) -> p c j", j=PACK)
+
+        def b_steps(parts):
+            g4, g5, big, res = {}, {}, {}, {}
+            for key in parts:
+                t, lo, hi = key
+                g4[key] = work.tile([P, hi - lo], F32, name="g4")
+                nc.vector.tensor_tensor(g4[key][:], b_win[t][:].indirect(entries(n4_sb, lo, hi)), b_plain[t][:, lo:hi], SUB)
+                g5[key] = work.tile([P, hi - lo], F32, name="g5")
+                nc.vector.tensor_tensor(g5[key][:], b_win[t][:].indirect(entries(n5_sb, lo, hi)), b_plain[t][:, lo:hi], SUB)
+            for key in parts:
+                t, lo, hi = key
+                big[key] = work.tile([P, hi - lo], F32, name="big")
+                nc.vector.tensor_tensor(big[key][:], g4[key][:], g5[key][:], MAX)
+            for key in parts:
+                t, lo, hi = key
+                res[key] = work.tile([P, hi - lo], F32, name="res")
+                nc.vector.tensor_tensor(res[key][:], b_win[t][:].indirect(entries(n3_sb, lo, hi)), big[key][:], SUB)
+                nc.scalar.activation(z2_view[:, lo:hi, t], res[key][:], COPY, scale=gi_sb[t][:])
+
+        b_steps(((0, 0, N), (1, 0, N)))
+        quantize(z_words, z_scales, z_bf, 0, H)
+        for piece in PIECES:
+            b_steps(((2,) + piece, (3,) + piece))
+
+        c_win = [keep.tile([P, 2 * N if t < 2 else N], F32, name=f"c_win{t}") for t in range(PACK)]
+        nc.gpsimd.memset(c_win[0][:, N:], 0.0)
+        c_rest = keep.tile([P, 3 * N], F32, name="c_rest")
+        c_plain = [c_win[1][:, N:], c_rest[:, :N], c_rest[:, N : 2 * N], c_rest[:, 2 * N :]]
+        acc0 = psum.tile([P, N], F32, name="acc_c0", tag="bank0")
+        for lo, hi in PIECES:
+            quantize(z2_words, z2_scales, z2_bf, lo, hi)
+            product(acc0, z_words, z_scales, 0, z2_words, z2_scales, lo, hi)
+            nc.scalar.activation(c_win[0][:, lo:hi], acc0[:, lo:hi], COPY, scale=0.75 * 0.0625)
+            nc.scalar.activation(c_plain[0][:, lo:hi], acc0[:, lo:hi], COPY, scale=0.0625)
+        for t in range(1, PACK):
+            acc = psum.tile([P, N], F32, name=f"acc_c{t}", tag=f"bank{t}")
+            product(acc, z_words, z_scales, t, z2_words, z2_scales, 0, N)
+            nc.scalar.activation(c_win[t][:, :N], acc[:], COPY, scale=0.75 * 0.0625)
+            nc.scalar.activation(c_plain[t], acc[:], COPY, scale=0.0625)
+
+        o_bf, o_words, o_scales = mx_tiles("o")
+        o_view = o_bf[:].rearrange("p (c j) -> p c j", j=PACK)
+        out_rows = out_0.rearrange("(p t) c -> p t c", t=PACK)
+        out_words = out_1[0].rearrange("p n t -> p (n t)").bitcast(I32)
+
+        def c_steps(pair, lo, hi, rounding):
+            tiles = (2 * pair, 2 * pair + 1)
+            g6 = {}
+            for t in tiles:
+                g6[t] = work.tile([P, hi - lo], F32, name="g6")
+                nc.vector.tensor_tensor(g6[t][:], c_win[t][:].indirect(entries(n6_sb, lo, hi)), c_plain[t][:, lo:hi], SUB)
+            y = keep.tile([P, 2, hi - lo], F32, name=f"y{pair}_{lo}")
+            for u, t in enumerate(tiles):
+                nc.vector.tensor_tensor(y[:, u, :], c_win[t][:].indirect(entries(n7_sb, lo, hi)), g6[t][:], ADD)
+            nc.sync.dma_start(out_rows[:, 2 * pair : 2 * pair + 2, lo:hi], y[:])
+            rounding(o_view[:, lo:hi, 2 * pair : 2 * pair + 2], y[:].rearrange("p u c -> p c u"))
+
+        c_steps(0, 0, N, nc.scalar.copy)
+        for lo, hi in PIECES:
+            c_steps(1, lo, hi, nc.vector.tensor_copy if hi == N else nc.scalar.copy)
+        for lo, hi in PIECES:
+            quantize(o_words, o_scales, o_bf, lo, hi)
+            nc.scalar.dma_start(out_words[:, lo:hi], o_words[:, lo:hi].bitcast(I32))
+        for q in range(4):
+            queue = nc.scalar if q % 2 else nc.sync
+            queue.dma_start(out_2[0, 4 * q : 4 * q + 4, :].bitcast(I32), o_scales[32 * q : 32 * q + 4, :].bitcast(I32))

@@ -1,6 +1,7 @@
 from contextlib import ExitStack
 
 import concourse.mybir as mybir
+from concourse.masks import make_identity
 
 K, T, S, H, N, W = 512, 2048, 512, 512, 512, 256
 FLOPS = 2 * K * S * H + 2 * K * S * N + 2 * S * H * N
@@ -15,8 +16,8 @@ FP8X4 = mybir.dt.float8_e4m3fn_x4
 ADD = mybir.AluOpType.add
 SUB = mybir.AluOpType.subtract
 MULT = mybir.AluOpType.mult
-MAX = mybir.AluOpType.max
 COPY = mybir.ActivationFunctionType.Copy
+RELU = mybir.ActivationFunctionType.Relu
 
 P = 128
 PACK = 4
@@ -28,7 +29,7 @@ def tile_picked_mombbondtrimlap_none_po_kernel(tc, x_words, x_scales, wa, wb, gt
     nc = tc.nc
     with ExitStack() as ctx:
         keep = ctx.enter_context(tc.tile_pool(name="keep", bufs=1))
-        work = ctx.enter_context(tc.tile_pool(name="work", bufs=2))
+        work = ctx.enter_context(tc.tile_pool(name="work", bufs=4))
         psum = ctx.enter_context(tc.psum_pool(name="psum", bufs=1))
 
         def load_list(name, src):
@@ -39,22 +40,24 @@ def tile_picked_mombbondtrimlap_none_po_kernel(tc, x_words, x_scales, wa, wb, gt
         def entries(tile, lo, hi):
             return tile[:, lo // LIST_ROWS : hi // LIST_ROWS]
 
-        xs = keep.tile([P, T], U8, name="xs")
-        for q in range(4):
-            rows = x_scales[0, 4 * q : 4 * q + 4, :].bitcast(I32)
-            nc.scalar.dma_start(xs[32 * q : 32 * q + 32, :].bitcast(I32), rows.unsqueeze(0).to_broadcast([8, 4, T // 4]))
-        offs_sb = load_list("offs_sb", offs)
         two_sb = load_list("two_sb", two)
-        wa_rows = wa.rearrange("(p j) c -> p j c", j=PACK)
-        wa_raw = [keep.tile([P, PACK, H // 2], F32, name=f"wa_raw{h}") for h in range(2)]
+        xs = keep.tile([P, T], U8, name="xs")
+        nc.vector.memset(xs[:].bitcast(I32), 0)
+        wb_rows = wb.rearrange("(p j) c -> p j c", j=PACK)
+        wb_raw = [keep.tile([P, PACK, N // 2], F32, name=f"wb_raw{h}") for h in range(2)]
         for h in range(2):
-            nc.sync.dma_start(wa_raw[h][:], wa_rows[:, :, h * (H // 2) : (h + 1) * (H // 2)])
+            nc.sync.dma_start(wb_raw[h][:], wb_rows[:, :, h * (N // 2) : (h + 1) * (N // 2)])
+            if h == 0:
+                for q in range(4):
+                    nc.sync.dma_start(xs[32 * q : 32 * q + 4, :].bitcast(I32), x_scales[0, 4 * q : 4 * q + 4, :].bitcast(I32))
+                offs_sb = load_list("offs_sb", offs)
         xw = keep.tile([P, T], I32, name="xw")
         nc.sync.dma_start(xw[:], x_words[0].rearrange("p n t -> p (n t)").bitcast(I32))
-        n1_sb = load_list("n1_sb", n1)
-        n2_sb = load_list("n2_sb", n2)
-        wb_raw = keep.tile([P, PACK, N], F32, name="wb_raw")
-        nc.sync.dma_start(wb_raw[:], wb.rearrange("(p j) c -> p j c", j=PACK))
+        n4_sb = load_list("n4_sb", n4)
+        n5_sb = load_list("n5_sb", n5)
+        n3_sb = load_list("n3_sb", n3)
+        wa_raw = keep.tile([P, PACK, H], F32, name="wa_raw", tag="wa_raw_then_sums", align_bytes=64)
+        nc.sync.dma_start(wa_raw[:], wa.rearrange("(p j) c -> p j c", j=PACK))
 
         def load_weights(name, src):
             tiles = []
@@ -65,13 +68,21 @@ def tile_picked_mombbondtrimlap_none_po_kernel(tc, x_words, x_scales, wa, wb, gt
                 tiles.append(tile)
             return tiles
 
-        gt_sb = load_weights("gt_sb", gt)
-        n4_sb = load_list("n4_sb", n4)
-        n5_sb = load_list("n5_sb", n5)
-        n3_sb = load_list("n3_sb", n3)
         gi_sb = load_weights("gi_sb", gi)
+        n1_sb = load_list("n1_sb", n1)
+        n2_sb = load_list("n2_sb", n2)
+        gt_sb = load_weights("gt_sb", gt)
         n6_sb = load_list("n6_sb", n6)
         n7_sb = load_list("n7_sb", n7)
+
+        wide = [keep.tile([P, 2 * N], F32, name=f"wide{t}") for t in range(PACK)]
+        for t in range(PACK):
+            nc.vector.memset(wide[t][:, N:], 0.0)
+        ident = keep.tile([P, P], F32, name="ident")
+        make_identity(nc, ident[:])
+        gi_neg = keep.tile([P, PACK], F32, name="gi_neg")
+        for t in range(PACK):
+            nc.scalar.activation(gi_neg[:, t : t + 1], gi_sb[t][:], COPY, scale=-1.0)
 
         def pick_scales(name, lst):
             got = keep.tile([P, S], U8, name=name + "_got")
@@ -120,100 +131,138 @@ def tile_picked_mombbondtrimlap_none_po_kernel(tc, x_words, x_scales, wa, wb, gt
             scales = keep.tile([P, N], U8, name=name + "_scales", align_bytes=64)
             return grouped, words, scales
 
-        xa_scales = pick_scales("xa_s", offs_sb)
-        xb_scales = pick_scales("xb_s", two_sb)
-        wa_bf, wa_words, wa_scales = mx_tiles("wa")
-        for h in range(2):
-            lo, hi = h * (H // 2), (h + 1) * (H // 2)
-            interleave(wa_bf[:, PACK * lo : PACK * hi], wa_raw[h][:])
-            quantize(wa_words, wa_scales, wa_bf, lo, hi)
-        xa_words = pick_words("xa_w", offs_sb)
-        xb_words = pick_words("xb_w", two_sb)
+        def bank(index, name):
+            return psum.tile([P, N], F32, name=name, tag=f"bank{index}")
 
+        def turn(acc, terms):
+            for c in range(N // P):
+                cols = slice(c * P, (c + 1) * P)
+                for i, term in enumerate(terms):
+                    nc.tensor.matmul(
+                        acc[:, cols], term[:, cols], ident[:], start=i == 0, stop=i == len(terms) - 1, is_transpose=True
+                    )
+
+        xb_scales = pick_scales("xb_s", two_sb)
+        xa_scales = pick_scales("xa_s", offs_sb)
+        wb_bf, wb_words, wb_scales = mx_tiles("wb")
+        for h in range(2):
+            lo, hi = h * (N // 2), (h + 1) * (N // 2)
+            interleave(wb_bf[:, PACK * lo : PACK * hi], wb_raw[h][:])
+            quantize(wb_words, wb_scales, wb_bf, lo, hi)
+        xb_words = pick_words("xb_w", two_sb)
+        xa_words = pick_words("xa_w", offs_sb)
+
+        half = N // 2
+        low, high = bank(0, "acc_b0_low"), bank(4, "acc_b0_high")
+        product(low, xb_words, xb_scales, 0, wb_words, wb_scales, 0, half)
+        product(high, xb_words, xb_scales, 0, wb_words, wb_scales, half, N)
+        nc.scalar.copy(wide[0][:, :half], low[:, :half])
+        nc.vector.tensor_copy(wide[0][:, half:N], high[:, half:])
+        for t in range(1, PACK):
+            acc = bank(t, f"acc_b{t}")
+            product(acc, xb_words, xb_scales, t, wb_words, wb_scales, 0, N)
+            nc.scalar.copy(wide[t][:, :N], acc[:])
+
+        wa_bf, wa_words, wa_scales = mx_tiles("wa", tag="wa_then_b4")
+        interleave(wa_bf[:], wa_raw[:])
+        z2_bf = keep.tile([P, PACK * N], BF16, name="z2_bf", align_bytes=64)
+        z2_view = z2_bf[:].rearrange("p (c j) -> p c j", j=PACK)
+
+        def b_gathers(tiles, b4):
+            rise, rest = {}, {}
+            for t in tiles:
+                nc.vector.tensor_copy(b4[:, t % 2, :], wide[t][:].indirect(n4_sb[:]))
+            for t in tiles:
+                rise[t] = work.tile([P, N], F32, name="rise")
+                nc.vector.tensor_tensor(rise[t][:], wide[t][:].indirect(n5_sb[:]), b4[:, t % 2, :], SUB)
+            for t in tiles:
+                rest[t] = work.tile([P, N], F32, name="rest")
+                nc.vector.tensor_tensor(rest[t][:], wide[t][:].indirect(n3_sb[:]), b4[:, t % 2, :], SUB)
+            return rise, rest
+
+        def b_sums(tiles, rise, rest, turned):
+            for t in tiles:
+                u = t % 2
+                acc = bank(2 * u, f"rise_t{t}")
+                turn(acc, [rise[t]])
+                nc.scalar.activation(turned[:, 2 * u, :], acc[:], RELU)
+            for t in tiles:
+                u = t % 2
+                acc = bank(2 * u + 1, f"rest_t{t}")
+                turn(acc, [wide[t], rest[t]])
+                nc.scalar.activation(turned[:, 2 * u + 1, :], acc[:], COPY, scale=-1.0)
+                acc = bank(2 * u, f"sum{t}")
+                turn(acc, [turned[:, 2 * u, :], turned[:, 2 * u + 1, :]])
+                nc.scalar.activation(z2_view[:, :, t], acc[:], COPY, scale=gi_neg[:, t : t + 1])
+
+        rise, rest = b_gathers((0, 1), keep.tile([P, 2, N], F32, name="b4_first"))
+        quantize(wa_words, wa_scales, wa_bf, 0, H)
         a_sb = [keep.tile([P, H], F32, name=f"a{t}") for t in range(PACK)]
         for t in range(PACK):
-            acc = psum.tile([P, H], F32, name=f"acc_a{t}", tag=f"bank{t}")
+            acc = bank(4 + t, f"acc_a{t}")
             product(acc, xa_words, xa_scales, t, wa_words, wa_scales, 0, H)
             nc.scalar.copy(a_sb[t][:], acc[:])
+        turned = keep.tile([P, PACK, N], F32, name="turned", tag="wa_raw_then_sums", align_bytes=64)
+        b_sums((0, 1), rise, rest, turned)
+        rise, rest = b_gathers((2, 3), keep.tile([P, 2, N], F32, name="b4_second", tag="wa_then_b4", align_bytes=64))
+        b_sums((2, 3), rise, rest, turned)
 
-        wb_bf, wb_words, wb_scales = mx_tiles("wb", tag="wb_then_pa")
-        interleave(wb_bf[:], wb_raw[:])
-        z_bf, z_words, z_scales = mx_tiles("z")
+        z_bf, z_words, z_scales = mx_tiles("z", tag="wa_raw_then_sums")
         z_view = z_bf[:].rearrange("p (t m j) -> p m t j", t=PACK, j=PACK)
 
         def a_pair(tiles):
             pa, pb, dt = {}, {}, {}
             for t in tiles:
-                if t == 2:
-                    pa[t] = keep.tile([P, W], F32, name="pa2", tag="wb_then_pa", align_bytes=64)
-                else:
-                    pa[t] = work.tile([P, W], F32, name="pa")
+                pa[t] = work.tile([P, W], F32, name="pa")
                 nc.vector.tensor_copy(pa[t][:], a_sb[t][:].indirect(n1_sb[:]))
-                pb[t] = work.tile([P, W], F32, name="pb")
+                pb[t] = keep.tile([P, W], F32, name=f"pb{t}", align_bytes=64)
                 nc.vector.tensor_copy(pb[t][:], a_sb[t][:].indirect(n2_sb[:]))
             for t in tiles:
                 dt[t] = work.tile([P, H], F32, name="dt")
                 nc.vector.tensor_tensor(dt[t][:].indirect(n1_sb[:]), pa[t][:], pb[t][:], ADD)
             for t in tiles:
                 nc.vector.tensor_tensor(dt[t][:].indirect(n2_sb[:]), pa[t][:], pb[t][:], MULT)
-            for t in tiles:
-                nc.scalar.activation(
-                    z_view[:, :, :, t], dt[t][:].rearrange("p (m t) -> p m t", t=PACK), COPY, scale=gt_sb[t][:]
-                )
+            return dt
 
-        a_pair((0, 1))
-        quantize(wb_words, wb_scales, wb_bf, 0, N)
-        b_win = [keep.tile([P, 2 * N if t < 2 else N], F32, name=f"b_win{t}") for t in range(PACK)]
-        b_rest = keep.tile([P, 2 * N], F32, name="b_rest")
-        b_plain = [b_win[1][:, N:], b_win[0][:, N:], b_rest[:, :N], b_rest[:, N:]]
+        def round_z(dt, t, lo, hi):
+            nc.scalar.activation(
+                z_view[:, :, lo:hi, t], dt[t][:].rearrange("p (m t) -> p m t", t=PACK)[:, :, lo:hi], COPY, scale=gt_sb[t][:]
+            )
+
+        dt = a_pair((0, 1))
+        round_z(dt, 0, 0, PACK)
+        round_z(dt, 1, 0, PACK)
+        dt = a_pair((2, 3))
+        round_z(dt, 2, 1, PACK)
+        for t in (2, 3):
+            nc.vector.tensor_scalar_mul(
+                z_view[:, :, 0, t], dt[t][:].rearrange("p (m t) -> p m t", t=PACK)[:, :, 0], gt_sb[t][:]
+            )
+        z2_words = keep.tile([P, N], U32, name="z2_words", tag="pb3", align_bytes=64)
+        z2_scales = keep.tile([P, N], U8, name="z2_scales", align_bytes=64)
+        quantize(z2_words, z2_scales, z2_bf, 0, half)
+
+        c_win = [wide[0], wide[1], keep.tile([P, N], F32, name="c_win2"), keep.tile([P, N], F32, name="c_win3")]
+        c_rest = keep.tile([P, PACK, N], F32, name="c_rest")
+        c_plain = [c_rest[:, t, :] for t in range(PACK)]
         for t in range(PACK):
-            acc = psum.tile([P, N], F32, name=f"acc_b{t}", tag=f"bank{4 + t}")
-            product(acc, xb_words, xb_scales, t, wb_words, wb_scales, 0, N)
-            nc.scalar.copy(b_win[t][:, :N], acc[:])
-            nc.scalar.copy(b_plain[t], acc[:])
-        a_pair((2, 3))
-
-        z2_bf, z2_words, z2_scales = mx_tiles("z2")
-        z2_view = z2_bf[:].rearrange("p (c j) -> p c j", j=PACK)
-
-        def b_steps(parts):
-            g4, g5, big, res = {}, {}, {}, {}
-            for key in parts:
-                t, lo, hi = key
-                g4[key] = work.tile([P, hi - lo], F32, name="g4")
-                nc.vector.tensor_tensor(g4[key][:], b_win[t][:].indirect(entries(n4_sb, lo, hi)), b_plain[t][:, lo:hi], SUB)
-                g5[key] = work.tile([P, hi - lo], F32, name="g5")
-                nc.vector.tensor_tensor(g5[key][:], b_win[t][:].indirect(entries(n5_sb, lo, hi)), b_plain[t][:, lo:hi], SUB)
-            for key in parts:
-                t, lo, hi = key
-                big[key] = work.tile([P, hi - lo], F32, name="big")
-                nc.vector.tensor_tensor(big[key][:], g4[key][:], g5[key][:], MAX)
-            for key in parts:
-                t, lo, hi = key
-                res[key] = work.tile([P, hi - lo], F32, name="res")
-                nc.vector.tensor_tensor(res[key][:], b_win[t][:].indirect(entries(n3_sb, lo, hi)), big[key][:], SUB)
-                nc.scalar.activation(z2_view[:, lo:hi, t], res[key][:], COPY, scale=gi_sb[t][:])
-
-        b_steps(((0, 0, N), (1, 0, N)))
-        quantize(z_words, z_scales, z_bf, 0, H)
-        for piece in PIECES:
-            b_steps(((2,) + piece, (3,) + piece))
-
-        c_win = [keep.tile([P, 2 * N if t < 2 else N], F32, name=f"c_win{t}") for t in range(PACK)]
-        nc.gpsimd.memset(c_win[0][:, N:], 0.0)
-        c_rest = keep.tile([P, 3 * N], F32, name="c_rest")
-        c_plain = [c_win[1][:, N:], c_rest[:, :N], c_rest[:, N : 2 * N], c_rest[:, 2 * N :]]
-        acc0 = psum.tile([P, N], F32, name="acc_c0", tag="bank0")
-        for lo, hi in PIECES:
-            quantize(z2_words, z2_scales, z2_bf, lo, hi)
-            product(acc0, z_words, z_scales, 0, z2_words, z2_scales, lo, hi)
-            nc.scalar.activation(c_win[0][:, lo:hi], acc0[:, lo:hi], COPY, scale=0.75 * 0.0625)
-            nc.scalar.activation(c_plain[0][:, lo:hi], acc0[:, lo:hi], COPY, scale=0.0625)
-        for t in range(1, PACK):
-            acc = psum.tile([P, N], F32, name=f"acc_c{t}", tag=f"bank{t}")
-            product(acc, z_words, z_scales, t, z2_words, z2_scales, 0, N)
-            nc.scalar.activation(c_win[t][:, :N], acc[:], COPY, scale=0.75 * 0.0625)
-            nc.scalar.activation(c_plain[t], acc[:], COPY, scale=0.0625)
+            if t > 0:
+                round_z(dt, 3, t, t + 1)
+            quantize(z_words, z_scales, z_bf, t * P, (t + 1) * P)
+            if t == 0:
+                quantize(z2_words, z2_scales, z2_bf, half, N)
+                low, high = bank(4, "acc_c0_low"), bank(0, "acc_c0_high")
+                product(low, z_words, z_scales, 0, z2_words, z2_scales, 0, half)
+                product(high, z_words, z_scales, 0, z2_words, z2_scales, half, N)
+                nc.vector.tensor_scalar_mul(c_win[0][:, :half], low[:, :half], 0.75 * 0.0625)
+                nc.scalar.activation(c_win[0][:, half:N], high[:, half:], COPY, scale=0.75 * 0.0625)
+                nc.vector.tensor_scalar_mul(c_plain[0][:, :half], low[:, :half], 0.0625)
+                nc.scalar.activation(c_plain[0][:, half:], high[:, half:], COPY, scale=0.0625)
+            else:
+                acc = bank(4 + t, f"acc_c{t}")
+                product(acc, z_words, z_scales, t, z2_words, z2_scales, 0, N)
+                nc.scalar.activation(c_win[t][:, :N], acc[:], COPY, scale=0.75 * 0.0625)
+                nc.scalar.activation(c_plain[t], acc[:], COPY, scale=0.0625)
 
         o_bf, o_words, o_scales = mx_tiles("o")
         o_view = o_bf[:].rearrange("p (c j) -> p c j", j=PACK)
@@ -225,7 +274,10 @@ def tile_picked_mombbondtrimlap_none_po_kernel(tc, x_words, x_scales, wa, wb, gt
             g6 = {}
             for t in tiles:
                 g6[t] = work.tile([P, hi - lo], F32, name="g6")
-                nc.vector.tensor_tensor(g6[t][:], c_win[t][:].indirect(entries(n6_sb, lo, hi)), c_plain[t][:, lo:hi], SUB)
+                for a, b in ((lo, half), (half, hi)) if t == 0 else ((lo, hi),):
+                    nc.vector.tensor_tensor(
+                        g6[t][:, a - lo : b - lo], c_win[t][:].indirect(entries(n6_sb, a, b)), c_plain[t][:, a:b], SUB
+                    )
             y = keep.tile([P, 2, hi - lo], F32, name=f"y{pair}_{lo}")
             for u, t in enumerate(tiles):
                 nc.vector.tensor_tensor(y[:, u, :], c_win[t][:].indirect(entries(n7_sb, lo, hi)), g6[t][:], ADD)
@@ -237,7 +289,8 @@ def tile_picked_mombbondtrimlap_none_po_kernel(tc, x_words, x_scales, wa, wb, gt
             c_steps(1, lo, hi, nc.vector.tensor_copy if hi == N else nc.scalar.copy)
         for lo, hi in PIECES:
             quantize(o_words, o_scales, o_bf, lo, hi)
-            nc.scalar.dma_start(out_words[:, lo:hi], o_words[:, lo:hi].bitcast(I32))
+            queue = nc.scalar if hi == N else nc.sync
+            queue.dma_start(out_words[:, lo:hi], o_words[:, lo:hi].bitcast(I32))
         for q in range(4):
             queue = nc.scalar if q % 2 else nc.sync
             queue.dma_start(out_2[0, 4 * q : 4 * q + 4, :].bitcast(I32), o_scales[32 * q : 32 * q + 4, :].bitcast(I32))

from contextlib import ExitStack

import concourse.mybir as mybir
from concourse.masks import make_identity

K, T, S, H, N, W = 512, 2048, 512, 512, 512, 256
FLOPS = 2 * K * S * H + 2 * K * S * N + 2 * S * H * N

F32 = mybir.dt.float32
BF16 = mybir.dt.bfloat16
I32 = mybir.dt.int32
U32 = mybir.dt.uint32
U16 = mybir.dt.uint16
U8 = mybir.dt.uint8
FP8X4 = mybir.dt.float8_e4m3fn_x4
ADD = mybir.AluOpType.add
SUB = mybir.AluOpType.subtract
MULT = mybir.AluOpType.mult
COPY = mybir.ActivationFunctionType.Copy
RELU = mybir.ActivationFunctionType.Relu

P = 128
PACK = 4
LIST_ROWS = 16
PIECES = ((0, 256), (256, 384), (384, 512))


def tile_picked_mombbondtrimlap_none_po_kernel(tc, x_words, x_scales, wa, wb, gt, gi, offs, two, n1, n2, n3, n4, n5, n6, n7, out_0, out_1, out_2):
    nc = tc.nc
    with ExitStack() as ctx:
        keep = ctx.enter_context(tc.tile_pool(name="keep", bufs=1))
        work = ctx.enter_context(tc.tile_pool(name="work", bufs=4))
        psum = ctx.enter_context(tc.psum_pool(name="psum", bufs=1))

        def load_list(name, src):
            tile = keep.tile(list(src.shape), U16, name=name)
            nc.sync.dma_start(tile[:], src)
            return tile

        def entries(tile, lo, hi):
            return tile[:, lo // LIST_ROWS : hi // LIST_ROWS]

        two_sb = load_list("two_sb", two)
        xs = keep.tile([P, T], U8, name="xs")
        nc.vector.memset(xs[:].bitcast(I32), 0)
        wb_rows = wb.rearrange("(p j) c -> p j c", j=PACK)
        wb_raw = [keep.tile([P, PACK, N // 2], F32, name=f"wb_raw{h}") for h in range(2)]
        for h in range(2):
            nc.sync.dma_start(wb_raw[h][:], wb_rows[:, :, h * (N // 2) : (h + 1) * (N // 2)])
            if h == 0:
                for q in range(4):
                    nc.sync.dma_start(xs[32 * q : 32 * q + 4, :].bitcast(I32), x_scales[0, 4 * q : 4 * q + 4, :].bitcast(I32))
                offs_sb = load_list("offs_sb", offs)
        xw = keep.tile([P, T], I32, name="xw")
        nc.sync.dma_start(xw[:], x_words[0].rearrange("p n t -> p (n t)").bitcast(I32))
        n4_sb = load_list("n4_sb", n4)
        n5_sb = load_list("n5_sb", n5)
        n3_sb = load_list("n3_sb", n3)
        wa_raw = keep.tile([P, PACK, H], F32, name="wa_raw", tag="wa_raw_then_sums", align_bytes=64)
        nc.sync.dma_start(wa_raw[:], wa.rearrange("(p j) c -> p j c", j=PACK))

        def load_weights(name, src):
            tiles = []
            for t in range(PACK):
                tile = keep.tile([P, 1], F32, name=f"{name}{t}")
                with nc.allow_non_contiguous_dma(reason="one weight for each partition"):
                    nc.sync.dma_start(tile[:], src.rearrange("(q t e) o -> t q e o", t=PACK, e=8)[t])
                tiles.append(tile)
            return tiles

        gi_sb = load_weights("gi_sb", gi)
        n1_sb = load_list("n1_sb", n1)
        n2_sb = load_list("n2_sb", n2)
        gt_sb = load_weights("gt_sb", gt)
        n6_sb = load_list("n6_sb", n6)
        n7_sb = load_list("n7_sb", n7)

        wide = [keep.tile([P, 2 * N], F32, name=f"wide{t}") for t in range(PACK)]
        for t in range(PACK):
            nc.vector.memset(wide[t][:, N:], 0.0)
        ident = keep.tile([P, P], F32, name="ident")
        make_identity(nc, ident[:])
        gi_neg = keep.tile([P, PACK], F32, name="gi_neg")
        for t in range(PACK):
            nc.scalar.activation(gi_neg[:, t : t + 1], gi_sb[t][:], COPY, scale=-1.0)

        def pick_scales(name, lst):
            got = keep.tile([P, S], U8, name=name + "_got")
            nc.vector.tensor_copy(got[:], xs[:].indirect(lst[:]))
            dealt = keep.tile([P, S], U8, name=name + "_dealt", align_bytes=64)
            nc.vector.tensor_copy(
                dealt[:].bitcast(I32).rearrange("p (t q w) -> p q t w", t=PACK, w=2),
                got[:].bitcast(I32).rearrange("p (q t w) -> p q t w", t=PACK, w=2),
            )
            return dealt

        def pick_words(name, lst):
            dealt = keep.tile([P, S], U32, name=name, align_bytes=64)
            nc.vector.tensor_copy(
                dealt[:].rearrange("p (t q e) -> p q t e", t=PACK, e=8),
                xw[:].bitcast(U32).indirect(lst[:]),
            )
            return dealt

        def interleave(dst, raw):
            nc.scalar.copy(
                dst.rearrange("p (c i j) -> p c j i", i=4, j=PACK),
                raw.rearrange("p j (c i) -> p c j i", i=4),
            )

        def quantize(words, scales, grouped, lo, hi):
            nc.vector.quantize_mx(
                out=words[:, lo:hi].bitcast(FP8X4), scales=scales[:, lo:hi], in_=grouped[:, PACK * lo : PACK * hi]
            )

        def product(acc, l_words, l_scales, t, r_words, r_scales, lo, hi):
            cols = slice(t * P, (t + 1) * P)
            nc.tensor.matmul_mx(
                out=acc[:, lo:hi],
                lhsT=l_words[:, cols].bitcast(FP8X4),
                lhsT_scale=l_scales[:, cols],
                rhs=r_words[:, lo:hi].bitcast(FP8X4),
                rhs_scale=r_scales[:, lo:hi],
                start=True,
                stop=True,
            )

        def mx_tiles(name, tag=None):
            grouped = keep.tile([P, PACK * N], BF16, name=name + "_bf", tag=tag or name + "_bf", align_bytes=64)
            words = keep.tile([P, N], U32, name=name + "_words", align_bytes=64)
            scales = keep.tile([P, N], U8, name=name + "_scales", align_bytes=64)
            return grouped, words, scales

        def bank(index, name):
            return psum.tile([P, N], F32, name=name, tag=f"bank{index}")

        def turn(acc, terms):
            for c in range(N // P):
                cols = slice(c * P, (c + 1) * P)
                for i, term in enumerate(terms):
                    nc.tensor.matmul(
                        acc[:, cols], term[:, cols], ident[:], start=i == 0, stop=i == len(terms) - 1, is_transpose=True
                    )

        xb_scales = pick_scales("xb_s", two_sb)
        xa_scales = pick_scales("xa_s", offs_sb)
        wb_bf, wb_words, wb_scales = mx_tiles("wb")
        for h in range(2):
            lo, hi = h * (N // 2), (h + 1) * (N // 2)
            interleave(wb_bf[:, PACK * lo : PACK * hi], wb_raw[h][:])
            quantize(wb_words, wb_scales, wb_bf, lo, hi)
        xb_words = pick_words("xb_w", two_sb)
        xa_words = pick_words("xa_w", offs_sb)

        half = N // 2
        low, high = bank(0, "acc_b0_low"), bank(4, "acc_b0_high")
        product(low, xb_words, xb_scales, 0, wb_words, wb_scales, 0, half)
        product(high, xb_words, xb_scales, 0, wb_words, wb_scales, half, N)
        nc.scalar.copy(wide[0][:, :half], low[:, :half])
        nc.vector.tensor_copy(wide[0][:, half:N], high[:, half:])
        for t in range(1, PACK):
            acc = bank(t, f"acc_b{t}")
            product(acc, xb_words, xb_scales, t, wb_words, wb_scales, 0, N)
            nc.scalar.copy(wide[t][:, :N], acc[:])

        wa_bf, wa_words, wa_scales = mx_tiles("wa", tag="wa_then_b4")
        interleave(wa_bf[:], wa_raw[:])
        z2_bf = keep.tile([P, PACK * N], BF16, name="z2_bf", align_bytes=64)
        z2_view = z2_bf[:].rearrange("p (c j) -> p c j", j=PACK)

        def b_gathers(tiles, b4):
            rise, rest = {}, {}
            for t in tiles:
                nc.vector.tensor_copy(b4[:, t % 2, :], wide[t][:].indirect(n4_sb[:]))
            for t in tiles:
                rise[t] = work.tile([P, N], F32, name="rise")
                nc.vector.tensor_tensor(rise[t][:], wide[t][:].indirect(n5_sb[:]), b4[:, t % 2, :], SUB)
            for t in tiles:
                rest[t] = work.tile([P, N], F32, name="rest")
                nc.vector.tensor_tensor(rest[t][:], wide[t][:].indirect(n3_sb[:]), b4[:, t % 2, :], SUB)
            return rise, rest

        def b_sums(tiles, rise, rest, turned):
            for t in tiles:
                u = t % 2
                acc = bank(2 * u, f"rise_t{t}")
                turn(acc, [rise[t]])
                nc.scalar.activation(turned[:, 2 * u, :], acc[:], RELU)
            for t in tiles:
                u = t % 2
                acc = bank(2 * u + 1, f"rest_t{t}")
                turn(acc, [wide[t], rest[t]])
                nc.scalar.activation(turned[:, 2 * u + 1, :], acc[:], COPY, scale=-1.0)
                acc = bank(2 * u, f"sum{t}")
                turn(acc, [turned[:, 2 * u, :], turned[:, 2 * u + 1, :]])
                nc.scalar.activation(z2_view[:, :, t], acc[:], COPY, scale=gi_neg[:, t : t + 1])

        rise, rest = b_gathers((0, 1), keep.tile([P, 2, N], F32, name="b4_first"))
        quantize(wa_words, wa_scales, wa_bf, 0, H)
        a_sb = [keep.tile([P, H], F32, name=f"a{t}") for t in range(PACK)]
        for t in range(PACK):
            acc = bank(4 + t, f"acc_a{t}")
            product(acc, xa_words, xa_scales, t, wa_words, wa_scales, 0, H)
            nc.scalar.copy(a_sb[t][:], acc[:])
        turned = keep.tile([P, PACK, N], F32, name="turned", tag="wa_raw_then_sums", align_bytes=64)
        b_sums((0, 1), rise, rest, turned)
        rise, rest = b_gathers((2, 3), keep.tile([P, 2, N], F32, name="b4_second", tag="wa_then_b4", align_bytes=64))
        b_sums((2, 3), rise, rest, turned)

        z_bf, z_words, z_scales = mx_tiles("z", tag="wa_raw_then_sums")
        z_view = z_bf[:].rearrange("p (t m j) -> p m t j", t=PACK, j=PACK)

        def a_pair(tiles):
            pa, pb, dt = {}, {}, {}
            for t in tiles:
                pa[t] = work.tile([P, W], F32, name="pa")
                nc.vector.tensor_copy(pa[t][:], a_sb[t][:].indirect(n1_sb[:]))
                pb[t] = keep.tile([P, W], F32, name=f"pb{t}", align_bytes=64)
                nc.vector.tensor_copy(pb[t][:], a_sb[t][:].indirect(n2_sb[:]))
            for t in tiles:
                dt[t] = work.tile([P, H], F32, name="dt")
                nc.vector.tensor_tensor(dt[t][:].indirect(n1_sb[:]), pa[t][:], pb[t][:], ADD)
            for t in tiles:
                nc.vector.tensor_tensor(dt[t][:].indirect(n2_sb[:]), pa[t][:], pb[t][:], MULT)
            return dt

        def round_z(dt, t, lo, hi):
            nc.scalar.activation(
                z_view[:, :, lo:hi, t], dt[t][:].rearrange("p (m t) -> p m t", t=PACK)[:, :, lo:hi], COPY, scale=gt_sb[t][:]
            )

        dt = a_pair((0, 1))
        round_z(dt, 0, 0, PACK)
        round_z(dt, 1, 0, PACK)
        dt = a_pair((2, 3))
        round_z(dt, 2, 1, PACK)
        for t in (2, 3):
            nc.vector.tensor_scalar_mul(
                z_view[:, :, 0, t], dt[t][:].rearrange("p (m t) -> p m t", t=PACK)[:, :, 0], gt_sb[t][:]
            )
        z2_words = keep.tile([P, N], U32, name="z2_words", tag="pb3", align_bytes=64)
        z2_scales = keep.tile([P, N], U8, name="z2_scales", align_bytes=64)
        quantize(z2_words, z2_scales, z2_bf, 0, half)

        c_win = [wide[0], wide[1], keep.tile([P, N], F32, name="c_win2"), keep.tile([P, N], F32, name="c_win3")]
        c_rest = keep.tile([P, PACK, N], F32, name="c_rest")
        c_plain = [c_rest[:, t, :] for t in range(PACK)]
        for t in range(PACK):
            if t > 0:
                round_z(dt, 3, t, t + 1)
            quantize(z_words, z_scales, z_bf, t * P, (t + 1) * P)
            if t == 0:
                quantize(z2_words, z2_scales, z2_bf, half, N)
                low, high = bank(4, "acc_c0_low"), bank(0, "acc_c0_high")
                product(low, z_words, z_scales, 0, z2_words, z2_scales, 0, half)
                product(high, z_words, z_scales, 0, z2_words, z2_scales, half, N)
                nc.vector.tensor_scalar_mul(c_win[0][:, :half], low[:, :half], 0.75 * 0.0625)
                nc.scalar.activation(c_win[0][:, half:N], high[:, half:], COPY, scale=0.75 * 0.0625)
                nc.vector.tensor_scalar_mul(c_plain[0][:, :half], low[:, :half], 0.0625)
                nc.scalar.activation(c_plain[0][:, half:], high[:, half:], COPY, scale=0.0625)
            else:
                acc = bank(4 + t, f"acc_c{t}")
                product(acc, z_words, z_scales, t, z2_words, z2_scales, 0, N)
                nc.scalar.activation(c_win[t][:, :N], acc[:], COPY, scale=0.75 * 0.0625)
                nc.scalar.activation(c_plain[t], acc[:], COPY, scale=0.0625)

        o_bf, o_words, o_scales = mx_tiles("o")
        o_view = o_bf[:].rearrange("p (c j) -> p c j", j=PACK)
        out_rows = out_0.rearrange("(p t) c -> p t c", t=PACK)
        out_words = out_1[0].rearrange("p n t -> p (n t)").bitcast(I32)

        def c_steps(pair, lo, hi, rounding):
            tiles = (2 * pair, 2 * pair + 1)
            g6 = {}
            for t in tiles:
                g6[t] = work.tile([P, hi - lo], F32, name="g6")
                for a, b in ((lo, half), (half, hi)) if t == 0 else ((lo, hi),):
                    nc.vector.tensor_tensor(
                        g6[t][:, a - lo : b - lo], c_win[t][:].indirect(entries(n6_sb, a, b)), c_plain[t][:, a:b], SUB
                    )
            y = keep.tile([P, 2, hi - lo], F32, name=f"y{pair}_{lo}")
            for u, t in enumerate(tiles):
                nc.vector.tensor_tensor(y[:, u, :], c_win[t][:].indirect(entries(n7_sb, lo, hi)), g6[t][:], ADD)
            nc.sync.dma_start(out_rows[:, 2 * pair : 2 * pair + 2, lo:hi], y[:])
            rounding(o_view[:, lo:hi, 2 * pair : 2 * pair + 2], y[:].rearrange("p u c -> p c u"))

        c_steps(0, 0, N, nc.scalar.copy)
        for lo, hi in PIECES:
            c_steps(1, lo, hi, nc.vector.tensor_copy if hi == N else nc.scalar.copy)
        for lo, hi in PIECES:
            quantize(o_words, o_scales, o_bf, lo, hi)
            queue = nc.scalar if hi == N else nc.sync
            queue.dma_start(out_words[:, lo:hi], o_words[:, lo:hi].bitcast(I32))
        for q in range(4):
            queue = nc.scalar if q % 2 else nc.sync
            queue.dma_start(out_2[0, 4 * q : 4 * q + 4, :].bitcast(I32), o_scales[32 * q : 32 * q + 4, :].bitcast(I32))
